import numpy as np
import ml_dtypes


def mxq(x, axis, fmt="e4m3"):
    dtype, down = {"e4m3": (ml_dtypes.float8_e4m3fn, 7), "e5m2": (ml_dtypes.float8_e5m2, 14)}[fmt]
    v = np.moveaxis(np.asarray(x, np.float32).astype(ml_dtypes.bfloat16).astype(np.float64), axis, -1)
    blocks = v.reshape(v.shape[:-1] + (-1, 32))
    amax = np.abs(blocks).max(-1, keepdims=True)
    byte = np.maximum(np.where(amax > 0, np.frexp(amax)[1] - 1 + 127, 0) - down, 1)
    scale = np.exp2(byte - 127.0)
    codes = (blocks / scale).astype(np.float32).astype(dtype).astype(np.float64)
    return np.moveaxis((codes * scale).reshape(v.shape), -1, axis)


WIDE = False


def mx_kscale(k):
    if not WIDE:
        return np.ones(k)
    levels = np.array([10, -10, 5, -5, 0])
    if k % 512:
        return np.exp2(np.random.permutation(np.resize(levels, k // 32))).repeat(32)
    a = np.empty((k // 512, 16))
    for p in range(k // 512):
        a[p, :8] = np.random.permutation(np.resize(levels, 8))
        for g in range(8):
            far = levels[np.abs(levels - a[p, g]) >= 10]
            a[p, g + 8] = far[np.random.randint(len(far))]
    return np.exp2(a.ravel()).repeat(32)


def f64(x):
    return np.asarray(x).astype(np.float64)


def striped(idx):
    return np.tile(idx.reshape(-1, 16).T, (8, 1)).astype(np.uint16)


def unstriped(offs):
    return offs[:16].T.reshape(-1).astype(np.int64)


K, T, E, C, N = 512, 2048, 16, 128, 512


def by_expert(wq, xq):
    return np.concatenate([wq[e].T @ xq[:, e * C:(e + 1) * C] for e in range(E)], axis=1)


def setup_inputs():
    n = np.random.standard_normal
    s = mx_kscale(K)[:, None]
    return {
        "xT": (n((K, T)) * s).astype(np.float32),
        "w": (n((E, K, N)) / np.sqrt(K) / s[None]).astype(np.float32),
        "gate": np.tile(np.random.uniform(0.2, 1.0, E * C), (N, 1)).astype(np.float32),
        "offs": striped(np.random.permutation(T)[:E * C]),
    }


def reference(xT, w, gate, offs):
    idx = unstriped(offs)
    xq = mxq(f64(xT)[:, idx], 0, "e4m3")
    y = by_expert(mxq(f64(w), 1, "e4m3"), xq)
    out = np.zeros((N, T))
    out[:, idx] = f64(gate) * y
    return out

@@ -1,0 +1,204 @@
+from contextlib import ExitStack
+
+import concourse.mybir as mybir
+
+K, T, E, C, N = 512, 2048, 16, 128, 512
+FLOPS = 2 * K * N * E * C
+
+F32 = mybir.dt.float32
+BF16 = mybir.dt.bfloat16
+U32 = mybir.dt.uint32
+U16 = mybir.dt.uint16
+U8 = mybir.dt.uint8
+FP8X4 = mybir.dt.float8_e4m3fn_x4
+MULT = mybir.AluOpType.mult
+
+P = 128
+PACK = 4
+NB = N // P
+HALF = 1024
+QUAD_SLOTS = 4 * C
+PAIR_SLOTS = 2 * C
+PAIRS = E // 2
+RAW_BUFS = 4
+TOKEN_SLICES = ((0, 256), (256, 512), (512, 1024), (1024, 1536), (1536, 2048))
+GATE_AFTER_W = {7: 1, 10: 2, 13: 3}
+TAIL = ((6, 0), (6, 1), (7, 0), (7, 1), (6, 2), (7, 2), (6, 3), (7, 3))
+
+
+def tile_routed_moe_kernel(tc, xT, w, gate, offs, out):
+    nc = tc.nc
+    with ExitStack() as ctx:
+        held = ctx.enter_context(tc.tile_pool(name="held", bufs=1))
+        wide = ctx.enter_context(tc.tile_pool(name="wide", bufs=4))
+        gathered = ctx.enter_context(tc.tile_pool(name="gathered", bufs=2))
+        sums_pool = ctx.enter_context(tc.tile_pool(name="sums_pool", bufs=5))
+        gates = ctx.enter_context(tc.tile_pool(name="gates", bufs=3))
+        raws = ctx.enter_context(tc.tile_pool(name="raws", bufs=RAW_BUFS))
+        wbs = ctx.enter_context(tc.tile_pool(name="wbs", bufs=3))
+        gbs = ctx.enter_context(tc.tile_pool(name="gbs", bufs=2))
+        psum = ctx.enter_context(tc.psum_pool(name="psum", bufs=8))
+
+        offsets = held.tile([P, T // 16], U16, name="offsets")
+        nc.sync.dma_start(offsets[:], offs)
+
+        tok_codes = held.tile([P, T], U32, name="tok_codes", align_bytes=64)
+        tok_scales = held.tile([P, T], U8, name="tok_scales", align_bytes=64)
+        w_codes = held.tile([P, E, N], U32, name="w_codes", align_bytes=64)
+        w_scales = held.tile([P, E, N], U8, name="w_scales", align_bytes=64)
+
+        x_planes = xT.rearrange("(p t) n -> p t n", t=PACK)
+        gate_blocks = gate.rearrange("(b p) j -> p b j", p=P)
+
+        planes = {}
+        raw_tiles = {}
+        wb_tiles = {}
+        gb_tiles = {}
+        gate_tiles = {}
+        bank_tiles = {}
+        sums_tiles = {}
+        windows = {}
+
+        def load_plane(t):
+            plane = wide.tile([P, T], F32, name="plane", tag="wide")
+            nc.sync.dma_start(plane[:], x_planes[:, t, :])
+            planes[t] = plane
+
+        def load_w(e):
+            raw = raws.tile([P, PACK, N], F32, name="raw", tag="raw")
+            nc.sync.dma_start(raw[:], w[e].rearrange("(p j) n -> p j n", j=PACK))
+            raw_tiles[e] = raw
+
+        def load_gate(q):
+            g = gates.tile([P, NB, QUAD_SLOTS], F32, name="gate_sb", tag="gate")
+            nc.sync.dma_start(g[:], gate_blocks[:, :, q * QUAD_SLOTS : (q + 1) * QUAD_SLOTS])
+            gate_tiles[q] = g
+
+        g4 = [gathered.tile([P, PACK, HALF], F32, name="g4", tag="g4") for h in range(2)]
+
+        def gather(t, h):
+            nc.vector.tensor_copy(
+                g4[h][:, t, :],
+                planes[t][:].indirect(offsets[:, h * HALF // 16 : (h + 1) * HALF // 16]),
+            )
+
+        def interleave_w(e):
+            pair, i = divmod(e, 2)
+            if i == 0:
+                wb = wbs.tile([P, 2, N, PACK], BF16, name="wb", tag="wb", align_bytes=64)
+                wb_tiles[pair] = wb
+            nc.scalar.copy(out=wb_tiles[pair][:, i, :, :], in_=raw_tiles[e][:].rearrange("p j n -> p n j"))
+            nxt = e + RAW_BUFS
+            if nxt < E:
+                load_w(nxt)
+                if nxt in GATE_AFTER_W:
+                    load_gate(GATE_AFTER_W[nxt])
+
+        def quantize_w(pair):
+            nc.vector.quantize_mx(
+                out=w_codes[:, 2 * pair : 2 * pair + 2, :].rearrange("p e n -> p (e n)").bitcast(FP8X4),
+                scales=w_scales[:, 2 * pair : 2 * pair + 2, :].rearrange("p e n -> p (e n)"),
+                in_=wb_tiles[pair][:].rearrange("p e n j -> p (e n j)"),
+            )
+
+        def slices_new_for(pair, done):
+            return [s for s in TOKEN_SLICES if s[0] < (pair + 1) * PAIR_SLOTS and s not in done]
+
+        def interleave_tokens(pair):
+            for a, b in slices_new_for(pair, gb_tiles):
+                h = a // HALF
+                gb = gbs.tile([P, b - a, PACK], BF16, name="gb", tag="gb", align_bytes=64)
+                nc.scalar.copy(
+                    out=gb[:],
+                    in_=g4[h][:, :, a - h * HALF : b - h * HALF].rearrange("p t n -> p n t"),
+                )
+                gb_tiles[(a, b)] = gb
+
+        quantized = []
+
+        def quantize_tokens(pair):
+            for a, b in slices_new_for(pair, quantized):
+                nc.vector.quantize_mx(
+                    out=tok_codes[:, a:b].bitcast(FP8X4),
+                    scales=tok_scales[:, a:b],
+                    in_=gb_tiles[(a, b)][:].rearrange("p n t -> p (n t)"),
+                )
+                quantized.append((a, b))
+
+        def multiply(pair):
+            for k in range(2):
+                bank = psum.tile([P, 2, PAIR_SLOTS], F32, name="bank", tag="bank")
+                bank_tiles[(pair, k)] = bank
+                for bb in range(2):
+                    feats = slice((2 * k + bb) * P, (2 * k + bb + 1) * P)
+                    for i in range(2):
+                        e = 2 * pair + i
+                        slots = slice(e * C, (e + 1) * C)
+                        nc.tensor.matmul_mx(
+                            out=bank[:, bb, i * C : (i + 1) * C],
+                            lhsT=w_codes[:, e, feats].bitcast(FP8X4),
+                            lhsT_scale=w_scales[:, e, feats],
+                            rhs=tok_codes[:, slots].bitcast(FP8X4),
+                            rhs_scale=tok_scales[:, slots],
+                            start=True,
+                            stop=True,
+                        )
+
+        def copy_sums(pair):
+            sums = sums_pool.tile([P, NB, PAIR_SLOTS], F32, name="sums", tag="sums")
+            sums_tiles[pair] = sums
+            for k in range(2):
+                nc.scalar.copy(out=sums[:, 2 * k : 2 * k + 2, :], in_=bank_tiles[(pair, k)][:])
+
+        def scatter(pair, b):
+            if b not in windows:
+                window = wide.tile([P, T], F32, name="window", tag="wide")
+                windows[b] = window
+            q, i = divmod(pair, 2)
+            nc.vector.tensor_tensor(
+                windows[b][:].indirect(offsets[:, pair * PAIR_SLOTS // 16 : (pair + 1) * PAIR_SLOTS // 16]),
+                sums_tiles[pair][:, b, :],
+                gate_tiles[q][:, b, i * PAIR_SLOTS : (i + 1) * PAIR_SLOTS],
+                MULT,
+            )
+
+        load_plane(0)
+        load_w(0)
+        load_plane(1)
+        load_w(1)
+        load_plane(2)
+        load_w(2)
+        load_w(3)
+        load_plane(3)
+        load_gate(0)
+
+        for t in range(3):
+            gather(t, 0)
+            gather(t, 1)
+            interleave_w(t)
+        interleave_w(3)
+        quantize_w(0)
+        gather(3, 0)
+        interleave_tokens(0)
+        gather(3, 1)
+        quantize_tokens(0)
+        multiply(0)
+        interleave_tokens(1)
+
+        for pair in range(PAIRS):
+            copy_sums(pair)
+            if pair + 2 < PAIRS:
+                interleave_w(2 * pair + 4)
+                interleave_w(2 * pair + 5)
+                interleave_tokens(pair + 2)
+            if pair + 1 < PAIRS:
+                quantize_w(pair + 1)
+                quantize_tokens(pair + 1)
+                multiply(pair + 1)
+            if pair < PAIRS - 2:
+                for b in range(NB):
+                    scatter(pair, b)
+        for pair, b in TAIL:
+            scatter(pair, b)
+            if pair == PAIRS - 1:
+                nc.sync.dma_start(out[b * P : (b + 1) * P, :], windows[b][:])

@@ -21,6 +21,7 @@ QUAD_SLOTS = 4 * C
 PAIR_SLOTS = 2 * C
 PAIRS = E // 2
 RAW_BUFS = 4
+RUN = 4
 TOKEN_SLICES = ((0, 256), (256, 512), (512, 1024), (1024, 1536), (1536, 2048))
 GATE_AFTER_W = {7: 1, 10: 2, 13: 3}
 TAIL = ((6, 0), (6, 1), (7, 0), (7, 1), (6, 2), (7, 2), (6, 3), (7, 3))
@@ -87,7 +88,10 @@ def tile_routed_moe_kernel(tc, xT, w, gate, offs, out):
             if i == 0:
                 wb = wbs.tile([P, 2, N, PACK], BF16, name="wb", tag="wb", align_bytes=64)
                 wb_tiles[pair] = wb
-            nc.scalar.copy(out=wb_tiles[pair][:, i, :, :], in_=raw_tiles[e][:].rearrange("p j n -> p n j"))
+            nc.scalar.copy(
+                out=wb_tiles[pair][:, i, :, :].rearrange("p (c i) j -> p c j i", i=RUN),
+                in_=raw_tiles[e][:].rearrange("p j (c i) -> p c j i", i=RUN),
+            )
             nxt = e + RAW_BUFS
             if nxt < E:
                 load_w(nxt)
@@ -109,8 +113,8 @@ def tile_routed_moe_kernel(tc, xT, w, gate, offs, out):
                 h = a // HALF
                 gb = gbs.tile([P, b - a, PACK], BF16, name="gb", tag="gb", align_bytes=64)
                 nc.scalar.copy(
-                    out=gb[:],
-                    in_=g4[h][:, :, a - h * HALF : b - h * HALF].rearrange("p t n -> p n t"),
+                    out=gb[:].rearrange("p (c i) t -> p c t i", i=RUN),
+                    in_=g4[h][:, :, a - h * HALF : b - h * HALF].rearrange("p t (c i) -> p c t i", i=RUN),
                 )
                 gb_tiles[(a, b)] = gb
 

@@ -20,7 +20,12 @@ HALF = 1024
 QUAD_SLOTS = 4 * C
 PAIR_SLOTS = 2 * C
 PAIRS = E // 2
-RAW_BUFS = 4
+STREAM_BUFS = 6
+LATER_LOADS = (
+    ("w", 5), ("w", 6), ("w", 7), ("g", 1), ("w", 8), ("w", 9), ("w", 10), ("w", 11),
+    ("g", 2), ("w", 12), ("w", 13), ("w", 14), ("w", 15), ("g", 3),
+)
+LAST_QUAD = 3
 RUN = 4
 TOKEN_SLICES = ((0, 256), (256, 512), (512, 1024), (1024, 1536), (1536, 2048))
 GATE_AFTER_W = {7: 1, 10: 2, 13: 3}
@@ -33,9 +38,9 @@ def tile_routed_moe_kernel(tc, xT, w, gate, offs, out):
         held = ctx.enter_context(tc.tile_pool(name="held", bufs=1))
         wide = ctx.enter_context(tc.tile_pool(name="wide", bufs=4))
         gathered = ctx.enter_context(tc.tile_pool(name="gathered", bufs=2))
-        sums_pool = ctx.enter_context(tc.tile_pool(name="sums_pool", bufs=5))
-        gates = ctx.enter_context(tc.tile_pool(name="gates", bufs=3))
-        raws = ctx.enter_context(tc.tile_pool(name="raws", bufs=RAW_BUFS))
+        sums_pool = ctx.enter_context(tc.tile_pool(name="sums_pool", bufs=3))
+        sums4_pool = ctx.enter_context(tc.tile_pool(name="sums4_pool", bufs=1))
+        stream = ctx.enter_context(tc.tile_pool(name="stream", bufs=STREAM_BUFS))
         wbs = ctx.enter_context(tc.tile_pool(name="wbs", bufs=3))
         gbs = ctx.enter_context(tc.tile_pool(name="gbs", bufs=2))
         psum = ctx.enter_context(tc.psum_pool(name="psum", bufs=8))
@@ -66,12 +71,12 @@ def tile_routed_moe_kernel(tc, xT, w, gate, offs, out):
             planes[t] = plane
 
         def load_w(e):
-            raw = raws.tile([P, PACK, N], F32, name="raw", tag="raw")
+            raw = stream.tile([P, PACK, N], F32, name="raw", tag="stream")
             nc.sync.dma_start(raw[:], w[e].rearrange("(p j) n -> p j n", j=PACK))
             raw_tiles[e] = raw
 
         def load_gate(q):
-            g = gates.tile([P, NB, QUAD_SLOTS], F32, name="gate_sb", tag="gate")
+            g = stream.tile([P, NB, QUAD_SLOTS], F32, name="gate_sb", tag="stream")
             nc.sync.dma_start(g[:], gate_blocks[:, :, q * QUAD_SLOTS : (q + 1) * QUAD_SLOTS])
             gate_tiles[q] = g
 
@@ -92,11 +97,12 @@ def tile_routed_moe_kernel(tc, xT, w, gate, offs, out):
                 out=wb_tiles[pair][:, i, :, :].rearrange("p (c i) j -> p c j i", i=RUN),
                 in_=raw_tiles[e][:].rearrange("p j (c i) -> p c j i", i=RUN),
             )
-            nxt = e + RAW_BUFS
-            if nxt < E:
-                load_w(nxt)
-                if nxt in GATE_AFTER_W:
-                    load_gate(GATE_AFTER_W[nxt])
+            if e < len(LATER_LOADS):
+                kind, index = LATER_LOADS[e]
+                if kind == "w":
+                    load_w(index)
+                else:
+                    load_gate(index)
 
         def quantize_w(pair):
             nc.vector.quantize_mx(
@@ -130,41 +136,71 @@ def tile_routed_moe_kernel(tc, xT, w, gate, offs, out):
                 quantized.append((a, b))
 
         def multiply(pair):
-            for k in range(2):
-                bank = psum.tile([P, 2, PAIR_SLOTS], F32, name="bank", tag="bank")
-                bank_tiles[(pair, k)] = bank
-                for bb in range(2):
-                    feats = slice((2 * k + bb) * P, (2 * k + bb + 1) * P)
-                    for i in range(2):
-                        e = 2 * pair + i
-                        slots = slice(e * C, (e + 1) * C)
-                        nc.tensor.matmul_mx(
-                            out=bank[:, bb, i * C : (i + 1) * C],
-                            lhsT=w_codes[:, e, feats].bitcast(FP8X4),
-                            lhsT_scale=w_scales[:, e, feats],
-                            rhs=tok_codes[:, slots].bitcast(FP8X4),
-                            rhs_scale=tok_scales[:, slots],
-                            start=True,
-                            stop=True,
-                        )
+            q, half = divmod(pair, 2)
+            for b in range(NB):
+                if q < LAST_QUAD:
+                    if b % 2 == 0:
+                        bank = psum.tile([P, 2, PAIR_SLOTS], F32, name="bank", tag="bank")
+                        bank_tiles[(pair, b // 2)] = bank
+                    dest = bank_tiles[(pair, b // 2)][:, b % 2, :]
+                else:
+                    if half == 0:
+                        bank4 = psum.tile([P, QUAD_SLOTS], F32, name="bank4", tag="bank")
+                        bank_tiles[("quad", q, b)] = bank4
+                    dest = bank_tiles[("quad", q, b)][:, half * PAIR_SLOTS : (half + 1) * PAIR_SLOTS]
+                feats = slice(b * P, (b + 1) * P)
+                for i in range(2):
+                    e = 2 * pair + i
+                    slots = slice(e * C, (e + 1) * C)
+                    nc.tensor.matmul_mx(
+                        out=dest[:, i * C : (i + 1) * C],
+                        lhsT=w_codes[:, e, feats].bitcast(FP8X4),
+                        lhsT_scale=w_scales[:, e, feats],
+                        rhs=tok_codes[:, slots].bitcast(FP8X4),
+                        rhs_scale=tok_scales[:, slots],
+                        start=True,
+                        stop=True,
+                    )
 
-        def copy_sums(pair):
+        def copy_sums_pair(pair):
             sums = sums_pool.tile([P, NB, PAIR_SLOTS], F32, name="sums", tag="sums")
             sums_tiles[pair] = sums
             for k in range(2):
                 nc.scalar.copy(out=sums[:, 2 * k : 2 * k + 2, :], in_=bank_tiles[(pair, k)][:])
 
-        def scatter(pair, b):
+        def copy_sums_quad(q):
+            sums4 = sums4_pool.tile([P, NB, QUAD_SLOTS], F32, name="sums4", tag="sums4")
+            sums_tiles[(q, "quad")] = sums4
+            for b in range(NB):
+                nc.scalar.copy(out=sums4[:, b, :], in_=bank_tiles[("quad", q, b)][:])
+
+        def window_of(b):
             if b not in windows:
                 window = wide.tile([P, T], F32, name="window", tag="wide")
                 windows[b] = window
+            return windows[b]
+
+        def scatter_pair(pair, b):
             q, i = divmod(pair, 2)
             nc.vector.tensor_tensor(
-                windows[b][:].indirect(offsets[:, pair * PAIR_SLOTS // 16 : (pair + 1) * PAIR_SLOTS // 16]),
+                window_of(b)[:].indirect(offsets[:, pair * PAIR_SLOTS // 16 : (pair + 1) * PAIR_SLOTS // 16]),
                 sums_tiles[pair][:, b, :],
                 gate_tiles[q][:, b, i * PAIR_SLOTS : (i + 1) * PAIR_SLOTS],
                 MULT,
             )
+
+        def scatter_quad(q, b):
+            nc.vector.tensor_tensor(
+                window_of(b)[:].indirect(offsets[:, q * QUAD_SLOTS // 16 : (q + 1) * QUAD_SLOTS // 16]),
+                sums_tiles[(q, "quad")][:, b, :],
+                gate_tiles[q][:, b, :],
+                MULT,
+            )
+
+        def prepare(pair):
+            quantize_w(pair)
+            quantize_tokens(pair)
+            multiply(pair)
 
         load_plane(0)
         load_w(0)
@@ -175,6 +211,7 @@ def tile_routed_moe_kernel(tc, xT, w, gate, offs, out):
         load_w(3)
         load_plane(3)
         load_gate(0)
+        load_w(4)
 
         for t in range(3):
             gather(t, 0)
@@ -189,20 +226,18 @@ def tile_routed_moe_kernel(tc, xT, w, gate, offs, out):
         multiply(0)
         interleave_tokens(1)
 
-        for pair in range(PAIRS):
-            copy_sums(pair)
+        for pair in range(PAIRS - 2):
+            copy_sums_pair(pair)
             if pair + 2 < PAIRS:
                 interleave_w(2 * pair + 4)
                 interleave_w(2 * pair + 5)
                 interleave_tokens(pair + 2)
-            if pair + 1 < PAIRS:
-                quantize_w(pair + 1)
-                quantize_tokens(pair + 1)
-                multiply(pair + 1)
-            if pair < PAIRS - 2:
-                for b in range(NB):
-                    scatter(pair, b)
-        for pair, b in TAIL:
-            scatter(pair, b)
-            if pair == PAIRS - 1:
-                nc.sync.dma_start(out[b * P : (b + 1) * P, :], windows[b][:])
+            prepare(pair + 1)
+            for b in range(NB):
+                scatter_pair(pair, b)
+                if pair == PAIRS - 3 and b == 1:
+                    prepare(PAIRS - 1)
+        copy_sums_quad(LAST_QUAD)
+        for b in range(NB):
+            scatter_quad(LAST_QUAD, b)
+            nc.sync.dma_start(out[b * P : (b + 1) * P, :], windows[b][:])

@@ -138,7 +138,7 @@ def tile_routed_moe_kernel(tc, xT, w, gate, offs, out):
         def multiply(pair):
             q, half = divmod(pair, 2)
             for b in range(NB):
-                if q < LAST_QUAD:
+                if q < LAST_QUAD or b < 2:
                     if b % 2 == 0:
                         bank = psum.tile([P, 2, PAIR_SLOTS], F32, name="bank", tag="bank")
                         bank_tiles[(pair, b // 2)] = bank
@@ -166,12 +166,13 @@ def tile_routed_moe_kernel(tc, xT, w, gate, offs, out):
             sums = sums_pool.tile([P, NB, PAIR_SLOTS], F32, name="sums", tag="sums")
             sums_tiles[pair] = sums
             for k in range(2):
-                nc.scalar.copy(out=sums[:, 2 * k : 2 * k + 2, :], in_=bank_tiles[(pair, k)][:])
+                if (pair, k) in bank_tiles:
+                    nc.scalar.copy(out=sums[:, 2 * k : 2 * k + 2, :], in_=bank_tiles[(pair, k)][:])
 
         def copy_sums_quad(q):
             sums4 = sums4_pool.tile([P, NB, QUAD_SLOTS], F32, name="sums4", tag="sums4")
             sums_tiles[(q, "quad")] = sums4
-            for b in range(NB):
+            for b in (2, 3):
                 nc.scalar.copy(out=sums4[:, b, :], in_=bank_tiles[("quad", q, b)][:])
 
         def window_of(b):
@@ -208,8 +209,8 @@ def tile_routed_moe_kernel(tc, xT, w, gate, offs, out):
         load_w(1)
         load_plane(2)
         load_w(2)
-        load_w(3)
         load_plane(3)
+        load_w(3)
         load_gate(0)
         load_w(4)
 
@@ -226,18 +227,19 @@ def tile_routed_moe_kernel(tc, xT, w, gate, offs, out):
         multiply(0)
         interleave_tokens(1)
 
-        for pair in range(PAIRS - 2):
+        for pair in range(PAIRS):
             copy_sums_pair(pair)
             if pair + 2 < PAIRS:
                 interleave_w(2 * pair + 4)
                 interleave_w(2 * pair + 5)
                 interleave_tokens(pair + 2)
-            prepare(pair + 1)
-            for b in range(NB):
+            if pair + 1 < PAIRS:
+                prepare(pair + 1)
+            for b in range(NB if pair < PAIRS - 2 else 2):
                 scatter_pair(pair, b)
-                if pair == PAIRS - 3 and b == 1:
-                    prepare(PAIRS - 1)
+                if pair == PAIRS - 1:
+                    nc.sync.dma_start(out[b * P : (b + 1) * P, :], windows[b][:])
         copy_sums_quad(LAST_QUAD)
-        for b in range(NB):
+        for b in (2, 3):
             scatter_quad(LAST_QUAD, b)
             nc.sync.dma_start(out[b * P : (b + 1) * P, :], windows[b][:])

@@ -22,9 +22,10 @@ PAIR_SLOTS = 2 * C
 PAIRS = E // 2
 STREAM_BUFS = 6
 LATER_LOADS = (
-    ("w", 5), ("w", 6), ("w", 7), ("g", 1), ("w", 8), ("w", 9), ("w", 10), ("w", 11),
-    ("g", 2), ("w", 12), ("w", 13), ("w", 14), ("w", 15), ("g", 3),
+    (("w", 4),), (("w", 5),), (("w", 6),), (("w", 7), ("g", 1)), (("w", 8),), (("w", 9),), (("w", 10),), (("w", 11),),
+    (("g", 2),), (("w", 12),), (("w", 13),), (("w", 14),), (("w", 15),), (("g", 3),),
 )
+SPLIT_EXPERT = 3
 LAST_QUAD = 3
 RUN = 4
 TOKEN_SLICES = ((0, 256), (256, 512), (512, 1024), (1024, 1536), (1536, 2048))
@@ -71,9 +72,13 @@ def tile_routed_moe_kernel(tc, xT, w, gate, offs, out):
             planes[t] = plane
 
         def load_w(e):
-            raw = stream.tile([P, PACK, N], F32, name="raw", tag="stream")
-            nc.sync.dma_start(raw[:], w[e].rearrange("(p j) n -> p j n", j=PACK))
-            raw_tiles[e] = raw
+            pieces = 2 if e == SPLIT_EXPERT else 1
+            width = N // pieces
+            raw_tiles[e] = []
+            for piece in range(pieces):
+                raw = stream.tile([P, PACK, width], F32, name="raw", tag="stream")
+                nc.sync.dma_start(raw[:], w[e].rearrange("(p j) n -> p j n", j=PACK)[:, :, piece * width : (piece + 1) * width])
+                raw_tiles[e].append(raw)
 
         def load_gate(q):
             g = stream.tile([P, NB, QUAD_SLOTS], F32, name="gate_sb", tag="stream")
@@ -93,16 +98,18 @@ def tile_routed_moe_kernel(tc, xT, w, gate, offs, out):
             if i == 0:
                 wb = wbs.tile([P, 2, N, PACK], BF16, name="wb", tag="wb", align_bytes=64)
                 wb_tiles[pair] = wb
-            nc.scalar.copy(
-                out=wb_tiles[pair][:, i, :, :].rearrange("p (c i) j -> p c j i", i=RUN),
-                in_=raw_tiles[e][:].rearrange("p j (c i) -> p c j i", i=RUN),
-            )
+            width = N // len(raw_tiles[e])
+            for piece, raw in enumerate(raw_tiles[e]):
+                nc.scalar.copy(
+                    out=wb_tiles[pair][:, i, piece * width : (piece + 1) * width, :].rearrange("p (c i) j -> p c j i", i=RUN),
+                    in_=raw[:].rearrange("p j (c i) -> p c j i", i=RUN),
+                )
             if e < len(LATER_LOADS):
-                kind, index = LATER_LOADS[e]
-                if kind == "w":
-                    load_w(index)
-                else:
-                    load_gate(index)
+                for kind, index in LATER_LOADS[e]:
+                    if kind == "w":
+                        load_w(index)
+                    else:
+                        load_gate(index)
 
         def quantize_w(pair):
             nc.vector.quantize_mx(
@@ -212,7 +219,6 @@ def tile_routed_moe_kernel(tc, xT, w, gate, offs, out):
         load_plane(3)
         load_w(3)
         load_gate(0)
-        load_w(4)
 
         for t in range(3):
             gather(t, 0)

@@ -12,6 +12,7 @@ U16 = mybir.dt.uint16
 U8 = mybir.dt.uint8
 FP8X4 = mybir.dt.float8_e4m3fn_x4
 MULT = mybir.AluOpType.mult
+COPY = mybir.ActivationFunctionType.Copy
 
 P = 128
 PACK = 4
@@ -27,6 +28,7 @@ LATER_LOADS = (
 )
 SPLIT_EXPERT = 3
 LAST_QUAD = 3
+S_FROM = 512
 RUN = 4
 TOKEN_SLICES = ((0, 256), (256, 512), (512, 1024), (1024, 1536), (1536, 2048))
 GATE_AFTER_W = {7: 1, 10: 2, 13: 3}
@@ -93,6 +95,13 @@ def tile_routed_moe_kernel(tc, xT, w, gate, offs, out):
                 planes[t][:].indirect(offsets[:, h * HALF // 16 : (h + 1) * HALF // 16]),
             )
 
+        def gather_part(t, a, b):
+            h = a // HALF
+            nc.vector.tensor_copy(
+                g4[h][:, t, a - h * HALF : b - h * HALF],
+                planes[t][:].indirect(offsets[:, a // 16 : b // 16]),
+            )
+
         def interleave_w(e):
             pair, i = divmod(e, 2)
             if i == 0:
@@ -125,10 +134,19 @@ def tile_routed_moe_kernel(tc, xT, w, gate, offs, out):
             for a, b in slices_new_for(pair, gb_tiles):
                 h = a // HALF
                 gb = gbs.tile([P, b - a, PACK], BF16, name="gb", tag="gb", align_bytes=64)
-                nc.scalar.copy(
-                    out=gb[:].rearrange("p (c i) t -> p c t i", i=RUN),
-                    in_=g4[h][:, :, a - h * HALF : b - h * HALF].rearrange("p t (c i) -> p c t i", i=RUN),
-                )
+                kept = PACK - 1 if a >= S_FROM else PACK
+                if a == 0:
+                    nc.vector.tensor_copy(
+                        gb[:].rearrange("p (c i) t -> p c t i", i=RUN),
+                        g4[h][:, :, a:b].rearrange("p t (c i) -> p c t i", i=RUN),
+                    )
+                else:
+                    nc.scalar.copy(
+                        out=gb[:, :, 0:kept].rearrange("p (c i) t -> p c t i", i=RUN),
+                        in_=g4[h][:, 0:kept, a - h * HALF : b - h * HALF].rearrange("p t (c i) -> p c t i", i=RUN),
+                    )
+                if a >= S_FROM:
+                    nc.scalar.activation(gb[:, :, 3], planes["xb"][:].indirect(offsets[:, a // 16 : b // 16]), COPY)
                 gb_tiles[(a, b)] = gb
 
         quantized = []
@@ -226,9 +244,12 @@ def tile_routed_moe_kernel(tc, xT, w, gate, offs, out):
             interleave_w(t)
         interleave_w(3)
         quantize_w(0)
-        gather(3, 0)
+        gather_part(3, 0, PAIR_SLOTS)
         interleave_tokens(0)
-        gather(3, 1)
+        gather_part(3, PAIR_SLOTS, S_FROM)
+        xb = held.tile([P, T], BF16, name="xb")
+        nc.scalar.copy(out=xb[:], in_=planes[3][:])
+        planes["xb"] = xb
         quantize_tokens(0)
         multiply(0)
         interleave_tokens(1)

@@ -21,14 +21,14 @@ HALF = 1024
 QUAD_SLOTS = 4 * C
 PAIR_SLOTS = 2 * C
 PAIRS = E // 2
-STREAM_BUFS = 6
+STREAM_BUFS = 5
 LATER_LOADS = (
-    (("w", 4),), (("w", 5),), (("w", 6),), (("w", 7), ("g", 1)), (("w", 8),), (("w", 9),), (("w", 10),), (("w", 11),),
-    (("g", 2),), (("w", 12),), (("w", 13),), (("w", 14),), (("w", 15),), (("g", 3),),
+    (("w", 4),), (("w", 5),), (("w", 6),), (("w", 7), ("g", 1), ("w", 8)), (("w", 9),), (("w", 10),), (("w", 11),), (("g", 2), ("w", 12)),
+    (("w", 13),), (("w", 14),), (("w", 15),), (("g", 3),),
 )
 SPLIT_EXPERT = 3
 LAST_QUAD = 3
-S_FROM = 512
+S_FROM = 1024
 RUN = 4
 TOKEN_SLICES = ((0, 256), (256, 512), (512, 1024), (1024, 1536), (1536, 2048))
 GATE_AFTER_W = {7: 1, 10: 2, 13: 3}
@@ -44,6 +44,7 @@ def tile_routed_moe_kernel(tc, xT, w, gate, offs, out):
         sums_pool = ctx.enter_context(tc.tile_pool(name="sums_pool", bufs=3))
         sums4_pool = ctx.enter_context(tc.tile_pool(name="sums4_pool", bufs=1))
         stream = ctx.enter_context(tc.tile_pool(name="stream", bufs=STREAM_BUFS))
+        gates = ctx.enter_context(tc.tile_pool(name="gates", bufs=2))
         wbs = ctx.enter_context(tc.tile_pool(name="wbs", bufs=3))
         gbs = ctx.enter_context(tc.tile_pool(name="gbs", bufs=2))
         psum = ctx.enter_context(tc.psum_pool(name="psum", bufs=8))
@@ -83,7 +84,7 @@ def tile_routed_moe_kernel(tc, xT, w, gate, offs, out):
                 raw_tiles[e].append(raw)
 
         def load_gate(q):
-            g = stream.tile([P, NB, QUAD_SLOTS], F32, name="gate_sb", tag="stream")
+            g = gates.tile([P, NB, QUAD_SLOTS], F32, name="gate_sb", tag="gate_sb")
             nc.sync.dma_start(g[:], gate_blocks[:, :, q * QUAD_SLOTS : (q + 1) * QUAD_SLOTS])
             gate_tiles[q] = g
 

@@ -29,7 +29,7 @@ LATER_LOADS = (
 SPLIT_EXPERT = 3
 LAST_QUAD = 3
 S_FROM = 1024
-RUN = 4
+RUN = 8
 TOKEN_SLICES = ((0, 256), (256, 512), (512, 1024), (1024, 1536), (1536, 2048))
 GATE_AFTER_W = {7: 1, 10: 2, 13: 3}
 TAIL = ((6, 0), (6, 1), (7, 0), (7, 1), (6, 2), (7, 2), (6, 3), (7, 3))

@@ -50,7 +50,6 @@ def tile_routed_moe_kernel(tc, xT, w, gate, offs, out):
         psum = ctx.enter_context(tc.psum_pool(name="psum", bufs=8))
 
         offsets = held.tile([P, T // 16], U16, name="offsets")
-        nc.sync.dma_start(offsets[:], offs)
 
         tok_codes = held.tile([P, T], U32, name="tok_codes", align_bytes=64)
         tok_scales = held.tile([P, T], U8, name="tok_scales", align_bytes=64)
@@ -230,6 +229,7 @@ def tile_routed_moe_kernel(tc, xT, w, gate, offs, out):
             multiply(pair)
 
         load_plane(0)
+        nc.sync.dma_start(offsets[:], offs)
         load_w(0)
         load_plane(1)
         load_w(1)

from contextlib import ExitStack

import concourse.mybir as mybir

K, T, E, C, N = 512, 2048, 16, 128, 512
FLOPS = 2 * K * N * E * C

F32 = mybir.dt.float32
BF16 = mybir.dt.bfloat16
U32 = mybir.dt.uint32
U16 = mybir.dt.uint16
U8 = mybir.dt.uint8
FP8X4 = mybir.dt.float8_e4m3fn_x4
MULT = mybir.AluOpType.mult
COPY = mybir.ActivationFunctionType.Copy

P = 128
PACK = 4
NB = N // P
HALF = 1024
QUAD_SLOTS = 4 * C
PAIR_SLOTS = 2 * C
PAIRS = E // 2
STREAM_BUFS = 5
LATER_LOADS = (
    (("w", 4),), (("w", 5),), (("w", 6),), (("w", 7), ("g", 1), ("w", 8)), (("w", 9),), (("w", 10),), (("w", 11),), (("g", 2), ("w", 12)),
    (("w", 13),), (("w", 14),), (("w", 15),), (("g", 3),),
)
SPLIT_EXPERT = 3
LAST_QUAD = 3
S_FROM = 1024
RUN = 8
TOKEN_SLICES = ((0, 256), (256, 512), (512, 1024), (1024, 1536), (1536, 2048))
GATE_AFTER_W = {7: 1, 10: 2, 13: 3}
TAIL = ((6, 0), (6, 1), (7, 0), (7, 1), (6, 2), (7, 2), (6, 3), (7, 3))


def tile_routed_moe_kernel(tc, xT, w, gate, offs, out):
    nc = tc.nc
    with ExitStack() as ctx:
        held = ctx.enter_context(tc.tile_pool(name="held", bufs=1))
        wide = ctx.enter_context(tc.tile_pool(name="wide", bufs=4))
        gathered = ctx.enter_context(tc.tile_pool(name="gathered", bufs=2))
        sums_pool = ctx.enter_context(tc.tile_pool(name="sums_pool", bufs=3))
        sums4_pool = ctx.enter_context(tc.tile_pool(name="sums4_pool", bufs=1))
        stream = ctx.enter_context(tc.tile_pool(name="stream", bufs=STREAM_BUFS))
        gates = ctx.enter_context(tc.tile_pool(name="gates", bufs=2))
        wbs = ctx.enter_context(tc.tile_pool(name="wbs", bufs=3))
        gbs = ctx.enter_context(tc.tile_pool(name="gbs", bufs=2))
        psum = ctx.enter_context(tc.psum_pool(name="psum", bufs=8))

        offsets = held.tile([P, T // 16], U16, name="offsets")

        tok_codes = held.tile([P, T], U32, name="tok_codes", align_bytes=64)
        tok_scales = held.tile([P, T], U8, name="tok_scales", align_bytes=64)
        w_codes = held.tile([P, E, N], U32, name="w_codes", align_bytes=64)
        w_scales = held.tile([P, E, N], U8, name="w_scales", align_bytes=64)

        x_planes = xT.rearrange("(p t) n -> p t n", t=PACK)
        gate_blocks = gate.rearrange("(b p) j -> p b j", p=P)

        planes = {}
        raw_tiles = {}
        wb_tiles = {}
        gb_tiles = {}
        gate_tiles = {}
        bank_tiles = {}
        sums_tiles = {}
        windows = {}

        def load_plane(t):
            plane = wide.tile([P, T], F32, name="plane", tag="wide")
            nc.sync.dma_start(plane[:], x_planes[:, t, :])
            planes[t] = plane

        def load_w(e):
            pieces = 2 if e == SPLIT_EXPERT else 1
            width = N // pieces
            raw_tiles[e] = []
            for piece in range(pieces):
                raw = stream.tile([P, PACK, width], F32, name="raw", tag="stream")
                nc.sync.dma_start(raw[:], w[e].rearrange("(p j) n -> p j n", j=PACK)[:, :, piece * width : (piece + 1) * width])
                raw_tiles[e].append(raw)

        def load_gate(q):
            g = gates.tile([P, NB, QUAD_SLOTS], F32, name="gate_sb", tag="gate_sb")
            nc.sync.dma_start(g[:], gate_blocks[:, :, q * QUAD_SLOTS : (q + 1) * QUAD_SLOTS])
            gate_tiles[q] = g

        g4 = [gathered.tile([P, PACK, HALF], F32, name="g4", tag="g4") for h in range(2)]

        def gather(t, h):
            nc.vector.tensor_copy(
                g4[h][:, t, :],
                planes[t][:].indirect(offsets[:, h * HALF // 16 : (h + 1) * HALF // 16]),
            )

        def gather_part(t, a, b):
            h = a // HALF
            nc.vector.tensor_copy(
                g4[h][:, t, a - h * HALF : b - h * HALF],
                planes[t][:].indirect(offsets[:, a // 16 : b // 16]),
            )

        def interleave_w(e):
            pair, i = divmod(e, 2)
            if i == 0:
                wb = wbs.tile([P, 2, N, PACK], BF16, name="wb", tag="wb", align_bytes=64)
                wb_tiles[pair] = wb
            width = N // len(raw_tiles[e])
            for piece, raw in enumerate(raw_tiles[e]):
                nc.scalar.copy(
                    out=wb_tiles[pair][:, i, piece * width : (piece + 1) * width, :].rearrange("p (c i) j -> p c j i", i=RUN),
                    in_=raw[:].rearrange("p j (c i) -> p c j i", i=RUN),
                )
            if e < len(LATER_LOADS):
                for kind, index in LATER_LOADS[e]:
                    if kind == "w":
                        load_w(index)
                    else:
                        load_gate(index)

        def quantize_w(pair):
            nc.vector.quantize_mx(
                out=w_codes[:, 2 * pair : 2 * pair + 2, :].rearrange("p e n -> p (e n)").bitcast(FP8X4),
                scales=w_scales[:, 2 * pair : 2 * pair + 2, :].rearrange("p e n -> p (e n)"),
                in_=wb_tiles[pair][:].rearrange("p e n j -> p (e n j)"),
            )

        def slices_new_for(pair, done):
            return [s for s in TOKEN_SLICES if s[0] < (pair + 1) * PAIR_SLOTS and s not in done]

        def interleave_tokens(pair):
            for a, b in slices_new_for(pair, gb_tiles):
                h = a // HALF
                gb = gbs.tile([P, b - a, PACK], BF16, name="gb", tag="gb", align_bytes=64)
                kept = PACK - 1 if a >= S_FROM else PACK
                if a == 0:
                    nc.vector.tensor_copy(
                        gb[:].rearrange("p (c i) t -> p c t i", i=RUN),
                        g4[h][:, :, a:b].rearrange("p t (c i) -> p c t i", i=RUN),
                    )
                else:
                    nc.scalar.copy(
                        out=gb[:, :, 0:kept].rearrange("p (c i) t -> p c t i", i=RUN),
                        in_=g4[h][:, 0:kept, a - h * HALF : b - h * HALF].rearrange("p t (c i) -> p c t i", i=RUN),
                    )
                if a >= S_FROM:
                    nc.scalar.activation(gb[:, :, 3], planes["xb"][:].indirect(offsets[:, a // 16 : b // 16]), COPY)
                gb_tiles[(a, b)] = gb

        quantized = []

        def quantize_tokens(pair):
            for a, b in slices_new_for(pair, quantized):
                nc.vector.quantize_mx(
                    out=tok_codes[:, a:b].bitcast(FP8X4),
                    scales=tok_scales[:, a:b],
                    in_=gb_tiles[(a, b)][:].rearrange("p n t -> p (n t)"),
                )
                quantized.append((a, b))

        def multiply(pair):
            q, half = divmod(pair, 2)
            for b in range(NB):
                if q < LAST_QUAD or b < 2:
                    if b % 2 == 0:
                        bank = psum.tile([P, 2, PAIR_SLOTS], F32, name="bank", tag="bank")
                        bank_tiles[(pair, b // 2)] = bank
                    dest = bank_tiles[(pair, b // 2)][:, b % 2, :]
                else:
                    if half == 0:
                        bank4 = psum.tile([P, QUAD_SLOTS], F32, name="bank4", tag="bank")
                        bank_tiles[("quad", q, b)] = bank4
                    dest = bank_tiles[("quad", q, b)][:, half * PAIR_SLOTS : (half + 1) * PAIR_SLOTS]
                feats = slice(b * P, (b + 1) * P)
                for i in range(2):
                    e = 2 * pair + i
                    slots = slice(e * C, (e + 1) * C)
                    nc.tensor.matmul_mx(
                        out=dest[:, i * C : (i + 1) * C],
                        lhsT=w_codes[:, e, feats].bitcast(FP8X4),
                        lhsT_scale=w_scales[:, e, feats],
                        rhs=tok_codes[:, slots].bitcast(FP8X4),
                        rhs_scale=tok_scales[:, slots],
                        start=True,
                        stop=True,
                    )

        def copy_sums_pair(pair):
            sums = sums_pool.tile([P, NB, PAIR_SLOTS], F32, name="sums", tag="sums")
            sums_tiles[pair] = sums
            for k in range(2):
                if (pair, k) in bank_tiles:
                    nc.scalar.copy(out=sums[:, 2 * k : 2 * k + 2, :], in_=bank_tiles[(pair, k)][:])

        def copy_sums_quad(q):
            sums4 = sums4_pool.tile([P, NB, QUAD_SLOTS], F32, name="sums4", tag="sums4")
            sums_tiles[(q, "quad")] = sums4
            for b in (2, 3):
                nc.scalar.copy(out=sums4[:, b, :], in_=bank_tiles[("quad", q, b)][:])

        def window_of(b):
            if b not in windows:
                window = wide.tile([P, T], F32, name="window", tag="wide")
                windows[b] = window
            return windows[b]

        def scatter_pair(pair, b):
            q, i = divmod(pair, 2)
            nc.vector.tensor_tensor(
                window_of(b)[:].indirect(offsets[:, pair * PAIR_SLOTS // 16 : (pair + 1) * PAIR_SLOTS // 16]),
                sums_tiles[pair][:, b, :],
                gate_tiles[q][:, b, i * PAIR_SLOTS : (i + 1) * PAIR_SLOTS],
                MULT,
            )

        def scatter_quad(q, b):
            nc.vector.tensor_tensor(
                window_of(b)[:].indirect(offsets[:, q * QUAD_SLOTS // 16 : (q + 1) * QUAD_SLOTS // 16]),
                sums_tiles[(q, "quad")][:, b, :],
                gate_tiles[q][:, b, :],
                MULT,
            )

        def prepare(pair):
            quantize_w(pair)
            quantize_tokens(pair)
            multiply(pair)

        load_plane(0)
        nc.sync.dma_start(offsets[:], offs)
        load_w(0)
        load_plane(1)
        load_w(1)
        load_plane(2)
        load_w(2)
        load_plane(3)
        load_w(3)
        load_gate(0)

        for t in range(3):
            gather(t, 0)
            gather(t, 1)
            interleave_w(t)
        interleave_w(3)
        quantize_w(0)
        gather_part(3, 0, PAIR_SLOTS)
        interleave_tokens(0)
        gather_part(3, PAIR_SLOTS, S_FROM)
        xb = held.tile([P, T], BF16, name="xb")
        nc.scalar.copy(out=xb[:], in_=planes[3][:])
        planes["xb"] = xb
        quantize_tokens(0)
        multiply(0)
        interleave_tokens(1)

        for pair in range(PAIRS):
            copy_sums_pair(pair)
            if pair + 2 < PAIRS:
                interleave_w(2 * pair + 4)
                interleave_w(2 * pair + 5)
                interleave_tokens(pair + 2)
            if pair + 1 < PAIRS:
                prepare(pair + 1)
            for b in range(NB if pair < PAIRS - 2 else 2):
                scatter_pair(pair, b)
                if pair == PAIRS - 1:
                    nc.sync.dma_start(out[b * P : (b + 1) * P, :], windows[b][:])
        copy_sums_quad(LAST_QUAD)
        for b in (2, 3):
            scatter_quad(LAST_QUAD, b)
            nc.sync.dma_start(out[b * P : (b + 1) * P, :], windows[b][:])
